import numpy as np, ml_dtypes
CORES = [40,64,80,88,96,104,120,144]
N = 8
import mx_ref
BF = ml_dtypes.bfloat16
def gentries(a):
    return np.ascontiguousarray(a.reshape(8, 16, -1).transpose(0, 2, 1)).reshape(8, -1)
def gtable(e):
    e = np.asarray(e); return np.ascontiguousarray(e.reshape(8, -1, 16).transpose(0, 2, 1)).reshape(128, -1).astype(np.int32)
def gcols(t, e):
    v = np.concatenate([t.reshape(8, 16, -1, 4), np.zeros((8, 16, 1, 4), BF)], axis=2)
    return np.ascontiguousarray(np.stack([v[g][:, e[g]] for g in range(8)])).reshape(128, -1)
def tile(rs):
    return np.stack(rs, axis=2).reshape(128, -1).astype(BF)
def pick(q, e):
    c = np.concatenate([q[0].reshape(128, -1, 4), np.zeros((128, 1, 4), np.uint8)], axis=1); s = np.concatenate([q[1], np.ones((16, 1), np.uint8)], axis=1)
    return (np.ascontiguousarray(c[:, e].reshape(128, -1)), np.ascontiguousarray(s[:, e]))
def join(*qs):
    return (np.concatenate([q[0] for q in qs], axis=1), np.concatenate([q[1] for q in qs], axis=1))
def put(q, e, v):
    c, s = q[0].reshape(128, -1, 4).copy(), q[1].copy(); c[:, e] = v[0].reshape(128, -1, 4); s[:, e] = v[1]
    return (c.reshape(128, -1), s)
def pk(c, s):
    return (np.ascontiguousarray(c), mx_ref.live(s))
def emit(q):
    return q[0], q[1]
def packed(v, rng):
    q = [mx_ref.quantize(np.ascontiguousarray(v[r])) for r in range(N)]
    return np.stack([a for a, b in q]), np.stack([mx_ref.plane(b, rng) for a, b in q])
def values_of_codes():
    e, c = np.zeros((128, 128, 4), np.float32), np.zeros((128, 2, 4), np.uint8)
    e[np.arange(128), np.arange(128), 0] = 1
    c[:127, :, 0] = np.arange(256).reshape(2, 128).T[:127]
    return mx_ref.matmul(mx_ref.quantize(e.reshape(128, 512).astype(BF)), (c.reshape(128, 8), np.full((16, 2), 127, np.uint8))).T.reshape(-1).astype(np.float64)
CODE_VALUE, SCALE_VALUE = values_of_codes(), 2.0 ** (np.arange(256) - 127.0)
def decode(q):
    return (CODE_VALUE[q[0]].reshape(16, 8, -1, 4) * SCALE_VALUE[q[1]][:, None, :, None] + 0.0).reshape(128, -1).astype(np.float32)
def f(rng, *shape):
    return mx_ref.flush((rng.standard_normal(shape, dtype=np.float32) * np.exp2(rng.integers(-2, 3, shape[:-1] + (1,)))).astype(BF))
def wide(rng, *shape, cols=0):
    v = rng.standard_normal(shape, dtype=np.float32) * np.exp2(rng.integers(-12, 13, shape)).astype(np.float32)
    if cols: v *= np.repeat(np.exp2(rng.integers(-cols, cols + 1, shape[:-2] + (1, shape[-1] // 4))) * (rng.random(shape[:-2] + (1, shape[-1] // 4)) > 0.0625), 4, axis=-1).astype(np.float32)
    return mx_ref.flush(v.astype(BF))
C, H = 288, 144
STEP = [4, 1, 2]
def numbers_of(rng):
    return {"x": np.array(f(rng, N, 128, 4 * C)), "u": np.array(f(rng, N, 128, 512)), "v": np.array(f(rng, N, 128, 512))}
def stored(m):
    return {"ml": np.stack([gtable(m[r]) for r in range(N)])}
def paired(e):
    m = np.zeros_like(e)
    np.put_along_axis(m, e, np.roll(e, H, axis=-1), axis=-1)
    return m
def pairings(rng):
    return paired(rng.permuted(np.tile(np.arange(C), (N, 8, 1)), axis=2))
def zigzag(rng, loop):
    s, t = rng.permutation(H), rng.permutation(H)
    a = np.concatenate([np.roll(t, -1), H + np.roll(s, -1)]).reshape(-1, 2)
    if not loop: a[H // 2 - 1, 1], a[-1, 0] = int(a[-1, 0]), int(a[H // 2 - 1, 1])
    b = np.concatenate([s, H + t]).reshape(-1, 2)
    return [paired(np.concatenate([k[:, 0], k[:, 1]])) for k in (a, b)]
def coil(rng):
    s = rng.permutation(H)
    k = np.concatenate([s, H + np.roll(s[:-1], -1), H + s[-1:]]).reshape(-1, 2)
    k[H // 2 - 1, 1], k[-1, 0] = int(k[-1, 0]), int(k[H // 2 - 1, 1])
    return paired(np.concatenate([k[:, 0], k[:, 1]]))
def layers(rng, still=[], pairs=False):
    w = np.array(f(rng, N, 128, 2048)).reshape(N, 8, 16, 4, 8, 16, 4)
    for i in still:
        w[:, :, i] = 0
        w[:, :, :, :, :, i] = 0
    if pairs:
        w[:, :, :, :, :, 8:] = 0
        for g in range(8):
            w[:, g, 8, 0, g, 8, 0] = -28.0
            for b in range(4): w[:, g, 10, b, g, 9, 0] = -2.0 ** (b - 5)
    return w
def weights(rng, w):
    c, s = packed(np.ascontiguousarray(w).reshape(N, 128, 2048), rng)
    return {"wc": c, "ws": s}
def setup_inputs(rng):
    return {**numbers_of(rng), **stored(pairings(rng)), **weights(rng, layers(rng))}
def setup_inputs_ties(rng):
    d = numbers_of(rng)
    o = rng.permutation(N)
    k = rng.integers(0, 4, (N, 8, C))
    k[o[0]] = 0
    k[o[1]] -= 4
    k[o[2]] = np.arange(C) < H
    kind = rng.permutation(8)
    m = np.zeros((N, 8, C), np.int64)
    for g in range(8):
        if 4 <= kind[g] < 7: k[:, g] = np.sort(k[:, g].reshape(N, 2, H), axis=1).reshape(N, C)
        for r in range(N):
            p, q = r ^ STEP[0], r ^ STEP[1]
            if kind[g] < 4 and r < p:
                a = zigzag(rng, kind[g] == 3)
                j = int(rng.integers(2))
                m[r, g], m[p, g] = a[j], a[1 - j]
            if 4 <= kind[g] < 6 and r < min(p, q, p ^ STEP[1]):
                m[r, g], m[q, g] = zigzag(rng, False)
                m[p, g] = m[p ^ STEP[1], g] = paired(np.arange(C))
            if kind[g] == 7: m[r, g] = paired(np.concatenate([rng.permutation(H), H + rng.permutation(H)]))
        if kind[g] == 6:
            m[:, g] = paired(np.arange(C))
            r = int(rng.integers(N))
            if STEP[0] ^ STEP[1] == STEP[2]: m[r, g] = coil(rng)
            else: m[r, g], m[r ^ STEP[2], g] = zigzag(rng, False)
    x = d["x"].reshape(N, 8, 16, C, 4)
    x[:, :, 0] = 0
    x[:, :, 0, :, 0] = k.astype(np.float32).astype(BF)
    a = np.exp2(rng.integers(-3, 4, (N, 8, 1)).astype(np.float32))
    x[:, :, 8:] = 0
    x[:, :, 8, :, 0] = (-1.125 * a).astype(BF)
    x[:, :, 10, :, 0] = (-0.0703125 * a).astype(BF)
    u = d["u"].reshape(N, 128, 128, 4)
    u[:, :, ::16] = 0
    for h in range(0, 128, 16): u[:, h, h, 0] = 1.0
    return {"x": x.reshape(N, 128, 4 * C), "u": u.reshape(N, 128, 512), "v": d["v"], **stored(twist(k, m)), **weights(rng, layers(rng, [0], True))}
def setup_inputs_near(rng):
    d = numbers_of(rng)
    x = d["x"].astype(np.float32).reshape(N, 8, 16, C, 4)
    x[:, :, 0] = 0
    x[:, :, 8:] = 0
    u = d["u"].reshape(N, 128, 128, 4)
    u[:, :, ::16] = 0
    w = layers(rng, [0, 8, 9, 10, 11, 12, 13, 14, 15])
    o = rng.permutation(N) % 4
    for r in range(N):
        c = rng.choice([-1.0, 1.0], (8, 1))
        s = rng.integers(0, 16, (8, C))
        digits = ((s[:, :, None] >> np.arange(4)) & 1) * np.exp2(np.arange(4) - 23.0)
        if o[r] < 2:
            x[r, :, 0, :, 0] = c
            x[r, :, 8] = digits
            x[r, :, 11, :, 0] = 2.0 ** -10
        elif o[r] == 2: x[r, :, 8] = digits * rng.choice([-1.0, 1.0], (8, C, 1))
        else:
            x[r, :, 8, :, 0] = np.where(s < 8, 1.25, 0.0) * 2.0 ** -30 * c
            x[r, :, 9, :, 0] = np.where(s < 8, 0.0, 1.125) * 2.0 ** -30 * c
            for g in rng.permutation(8)[:4]:
                e = rng.choice([-1.0, 1.0], C) * 2.0 ** -30
                x[r, g, 8, :, 0] = 1.25 * e
                x[r, g, 9, :, 0] = -1.125 * e
            for g in range(8):
                w[r, g, 8, 0, g, 12, 0] = 2.0 ** -8
                w[r, g, 8, 0, g, 14, 0] = 64.0
                w[r, g, 1, 0, g, 2, 0] = 256.0
        at = [0, C - 1, int(rng.integers(C)), int(rng.integers(C))]
        for g, j in zip(rng.permutation(8)[:4], at): x[r, g, 0, j, 0] = 2.0 ** 29 * rng.choice([-1.0, 1.0])
        k = 1.0 if o[r] == 0 else 2.0 ** -30
        for h in range(0, 128, 16):
            u[r, h, h, 0] = k if o[r] < 2 else 1.0
            if o[r] < 2: u[r, h + 11, h, 0] = k
            if o[r] < 3: u[r, h + 8, h] = k
            else:
                u[r, h + 8, h, 0] = k
                u[r, h + 9, h, 0] = 1.125 * k
                u[r, h + 12, h, 0] = k
    return {"x": x.reshape(N, 128, 4 * C).astype(BF), "u": u.reshape(N, 128, 512), "v": d["v"], **stored(pairings(rng)), **weights(rng, w)}
def setup_inputs_odd(rng):
    d = numbers_of(rng)
    x = (1.0 + (2 * rng.integers(0, 64, (N, 16, 8, C, 4)) + 1) * 2.0 ** -7) * np.exp2(-rng.integers(0, 7, (N, 16, 8, C, 4)).astype(np.float64)) * rng.choice([-1.0, 1.0], (N, 16, 8, C, 4))
    x[:, :, 0, :, 0] = 1.96875 * 2.0 ** 8 * rng.choice([-1.0, 1.0], (N, 16, C))
    u = d["u"].reshape(N, 16, 8, 128, 4)
    u[:, :, 0, ::16] = 0
    for r in range(N):
        for i, g in enumerate(rng.permutation(8)[:4]):
            x[r, 2 * g, 1, :, 0] = (8 + rng.integers(0, 2, C)) * 2.0 ** (i - 8)
            u[r, :, :, 16 * g] = 0
            u[r, 2 * g, 1, 16 * g, 0] = 1.0
    return {"x": x.astype(np.float32).reshape(N, 128, 4 * C).astype(BF), "u": u.reshape(N, 128, 512), "v": d["v"], **stored(pairings(rng)), **weights(rng, layers(rng, [0, 8]))}
def setup_inputs_ends(rng):
    d = numbers_of(rng)
    x = np.zeros((N, 8, 16, C, 4))
    u = d["u"].astype(np.float32).reshape(N, 128, 128, 4)
    v = d["v"].astype(np.float32)
    w = np.zeros((N, 128, 4, 128, 4), np.float32)
    m = pairings(rng)
    o, e = rng.permutation(N) % 4, rng.permutation(N) % 4
    i = np.arange(128)
    for r in range(N):
        h = rng.permutation(8)
        c = np.where(h < 2, 0.0, h % 2 * 2.0 - 1.0)[None, :, None]
        k = np.array([2.0, 4.0, -4.0])[rng.permutation(8) % 3]
        low = -(0.9 + 0.1 * rng.random((8, 16, C, 4))) * 2.0 ** 28
        if o[r] == 0: x[r] = low
        if o[r] == 1: x[r] = low * rng.choice([-1.0, 1.0], (C, 1))
        if o[r] < 2:
            u[r, :, ::16] = c * (0.9 + 0.1 * rng.random((128, 8, 4))) * 2.0 ** 30
            v[r] = rng.choice([-1.0, 1.0], (128, 512)) * (0.9 + 0.1 * rng.random((128, 512))) * 2.0 ** 30
        if o[r] == 2:
            x[r] = -(1.0 + 0.125 * rng.integers(0, 8, (8, 16, C, 4))) * 2.0 ** -30
            u[r, :, ::16] = c * (1.0 + 0.125 * rng.integers(0, 8, (128, 8, 4))) * 2.0 ** -30
            v[r] = rng.choice([-1.0, 1.0], (128, 512)) * (1.0 + 0.125 * rng.integers(0, 8, (128, 512))) * 2.0 ** -30
            k[:] = 32.0
        if o[r] == 3:
            x[r] = d["x"][r].astype(np.float32).reshape(8, 16, C, 4)[:, :, :1]
            u[r, :, ::16] *= np.abs(c).astype(np.float32)
        for b in range(4): w[r, i, b, i, b] = k[i // 16]
        if e[r] < 3: m[r] = [paired(np.arange(C)), np.arange(C) ^ 1, C - 1 - np.arange(C)][e[r]]
    return {"x": x.astype(np.float32).reshape(N, 128, 4 * C).astype(BF), "u": u.reshape(N, 128, 512).astype(BF), "v": v.astype(BF), **stored(m), **weights(rng, w.astype(BF))}
def setup_inputs_spread(rng):
    d = setup_inputs(rng)
    d["x"] = wide(rng, N, 128, 4 * C, cols=6)
    return d
def check_inputs(d):
    b = []
    for k in ("x", "u", "v"):
        a = np.abs(d[k].astype(np.float32))
        if not (np.isfinite(a).all() and ((a == 0) | (a >= 2.0 ** -30) & (a <= 2.0 ** 30)).all()): b.append("a value of " + k)
    none, least, most = [emit(mx_ref.quantize(np.full((128, 16), k, np.float32).astype(BF)))[1][0, 0] for k in (0.0, 2.0 ** -8, 2.0 ** 8)]
    for r in range(N):
        e = gentries(d["ml"][r]).astype(np.int64)
        if not ((e >= 0) & (e < C)).all(): b.append("an entry of ml")
        elif (e == np.arange(C)).any() or (np.take_along_axis(e, e, axis=1) != np.arange(C)).any(): b.append("ml: not a pairing")
        if ((d["wc"][r] == 0x7F) | (d["wc"][r] == 0xFF)).any(): b.append("wc: a code that is no number")
        s = mx_ref.live(d["ws"][r])
        if ((s != none) & ((s < least) | (s > most))).any(): b.append("ws: a scale out of range")
    return b
def twist(s, m):
    e = np.zeros(m.shape, np.int64) + np.arange(C)
    swap = H * (s[..., :H] > s[..., H:])
    e[..., :H] += swap
    e[..., H:] -= swap
    return np.take_along_axis(e, np.take_along_axis(m, e, axis=-1), axis=-1)
def glued(a, b):
    at = np.tile(np.arange(C), (8, 1))
    far = at >= H
    done = np.zeros((8, C), bool)
    for _ in range(H + 1):
        at = np.where(done, at, np.where(far, np.take_along_axis(b, at, axis=1), np.take_along_axis(a, at, axis=1)))
        done = done | ((at >= H) == far)
        at = np.where(done, at, np.where(far, at + H, at - H))
        far = far ^ ~done
        if done.all(): break
    return at
def plus(s, t):
    return (s.astype(np.float32) + t.astype(np.float32)).astype(BF)
def reference(x, u, v, ml, wc, ws):
    qu = [mx_ref.quantize(u[r]) for r in range(N)]
    lay = [pk(wc[r], ws[r]) for r in range(N)]
    now = [x[r] for r in range(N)]
    mate = [gentries(ml[r]).astype(np.int64) for r in range(N)]
    for step in STEP:
        turned, qa = [], []
        for r in range(N):
            s = mx_ref.matmul(qu[r], mx_ref.quantize(now[r]))[::16] + np.float32(0.0)
            turned.append(twist(s, mate[r]))
            qz = mx_ref.quantize(plus(now[r], gcols(now[r], turned[r])))
            qa.append(mx_ref.quantize(tile([mx_ref.matmul(pick(lay[r], np.arange(128 * b, 128 * b + 128)), qz) * np.float32(0.015625) for b in range(4)])))
        made = []
        for r in range(N):
            p = r ^ step
            mate[r] = glued(turned[r], turned[p])
            t = decode(join(pick(qa[r], np.arange(H)), pick(qa[p], np.arange(H, C)))).astype(BF)
            made.append(plus(now[r], gcols(t, mate[r])))
        now = made
    y, mo = np.zeros((N, 128, C), np.float32), np.zeros((N, 8, C), np.float32)
    oc, osc = np.zeros((N, 128, 4 * C), np.uint8), np.zeros((N, 16, C), np.uint8)
    for r in range(N):
        q = mx_ref.quantize(now[r])
        y[r] = mx_ref.matmul(mx_ref.quantize(v[r]), q)
        mo[r] = mate[r]
        oc[r], osc[r] = emit(q)
    return {"y": y, "mo": mo, "oc": oc, "osc": osc}

from concourse.bass import DstId, RemoteDMATransfer
from concourse.mybir import dt, AluOpType, ActivationFunctionType

C, H = 288, 144
STEP = (4, 1, 2)
AW, MID = 432, 216
ROUNDS = len(STEP)

SCRATCH = {}
for _n in ("x0", "x1", "x2", "x3", "z", "a"):
    SCRATCH[_n] = ("sbuf", [128, 4 * C], "bfloat16")
for _n in ["x", "z"] + ["a%d" % i for i in range(ROUNDS)]:
    SCRATCH["q" + _n] = ("sbuf", [128, C], "float8_e4m3fn_x4")
    SCRATCH["s" + _n] = ("sbuf", [128, C], "uint8")
for _n in range(ROUNDS):
    SCRATCH["qp%d" % _n] = ("sbuf", [128, H], "float8_e4m3fn_x4")
    SCRATCH["sp%d" % _n] = ("sbuf", [128, H], "uint8")
    SCRATCH["lu%d" % _n] = ("sbuf", [128, 10], "uint16")
    SCRATCH["ll%d" % _n] = ("sbuf", [128, 10], "uint16")
    SCRATCH["na%d" % _n] = ("sbuf", [128, 20], "uint16")
for _n in ("u", "v"):
    SCRATCH[_n + "t"] = ("sbuf", [128, 512], "bfloat16")
for _n in ("u", "r", "v"):
    SCRATCH["q" + _n] = ("sbuf", [128, 128], "float8_e4m3fn_x4")
    SCRATCH["s" + _n] = ("sbuf", [128, 128], "uint8")
for _n in ("w", "e"):
    SCRATCH["q" + _n] = ("sbuf", [128, 512], "float8_e4m3fn_x4")
    SCRATCH["s" + _n] = ("sbuf", [128, 512], "uint8")
SCRATCH.update({
    "et": ("sbuf", [128, 2048], "bfloat16"),
    "ones": ("sbuf", [128, 128], "bfloat16"),
    "idn": ("sbuf", [128, 128], "bfloat16"),
    "mli": ("sbuf", [128, 18], "int32"),
    "mlf": ("sbuf", [128, 20], "float32"),
    "mlg": ("sbuf", [128, 20], "float32"),
    "mlh": ("sbuf", [128, 20], "float32"),
    "mli2": ("sbuf", [128, 20], "float32"),
    "lm": ("sbuf", [128, 28], "uint16"),
    "mm": ("sbuf", [128, 20], "float32"),
    "mt": ("sbuf", [128, 20], "float32"),
    "w1": ("sbuf", [128, 20], "float32"),
    "d1": ("sbuf", [128, 10], "float32"),
    "e1": ("sbuf", [128, 10], "float32"),
    "nn": ("sbuf", [128, 20], "float32"),
    "xp": ("sbuf", [128, 4 * C], "bfloat16"),
    "fl": ("sbuf", [128, AW], "bfloat16"),
    "scu": ("sbuf", [128, H], "float32"),
    "mgt": ("sbuf", [128, 448], "bfloat16"),
    "sct": ("sbuf", [128, 448], "bfloat16"),
    "mskt": ("sbuf", [128, 448], "bfloat16"),
    "rst": ("sbuf", [128, 448], "bfloat16"),
    "msk": ("sbuf", [128, 304], "bfloat16"),
    "mg": ("sbuf", [128, 304], "bfloat16"),
    "sc": ("sbuf", [128, 304], "bfloat16"),
    "h": ("sbuf", [128, C], "bfloat16"),
    "up": ("sbuf", [128, C], "bfloat16"),
    "vtab": ("sbuf", [128, C], "bfloat16"),
    "ta": ("sbuf", [128, AW], "bfloat16"),
    "tb": ("sbuf", [128, AW], "bfloat16"),
    "tc": ("sbuf", [128, AW], "bfloat16"),
    "gtb": ("sbuf", [128, AW], "float32"),
    "lk0": ("sbuf", [128, 10], "uint16"),
    "lk1": ("sbuf", [128, 10], "uint16"),
    "db": ("sbuf", [128, 4 * AW], "bfloat16"),
    "mrow": ("sbuf", [128, 304], "float32"),
    "ys": ("sbuf", [128, C], "float32"),
    "iom": ("sbuf", [128, 448], "int32"),
    "ioa": ("sbuf", [128, 448], "int32"),
    "ul": ("sbuf", [128, 8], "int32"),
    "uo": ("sbuf", [128, 8], "uint16"),
    "pc": ("sbuf", [128, 9], "int32"),
    "pd": ("sbuf", [128, 9], "int32"),
    "k16": ("sbuf", [128, 9], "int32"),
    "idl": ("sbuf", [128, 9], "int32"),
    "ps": ("psum", [128, 4096], "float32"),
})
LOADS = ["ldxu", "ldxl", "ldu", "ldm", "ldw", "lds", "ldv"]
STORES = ["sty0", "sty1", "stc0", "stc1", "sts0", "sts1", "sts2", "sts3", "stm0", "stm1"]
SEMAPHORES = (["ve", "ac", "pe", "gp", "out"] + LOADS + STORES
              + [n + "%d" % i for n in ("lu", "ll", "qp", "sp") for i in range(ROUNDS)])


def relays(topo, src, dst):
    ks = [k for k in topo.cores_of(src) if k != src and topo.may_write(k, dst)]
    return sorted(ks, key=lambda k: (topo.die(k) != topo.die(src), k))[:2]


def bits(es):
    return sum(1 << e for e in es)


def chip_masks(topo, src, rl):
    e = topo.engines(src, rl[0])
    f = topo.engines(src, rl[1])
    n = len(e) // 2
    return [e[:n], [k for k in f if k not in e[:n]][:n]]


def relay_program(g, core, T, topo):
    home = [r for r, c in enumerate(T.cores) if core in topo.cores_of(c)]
    if not home:
        return
    r = home[0]
    src = T.cores[r]
    sent = 0
    for i, s in enumerate(STEP):
        dst = T.cores[r ^ s]
        rl = relays(topo, src, dst)
        if core not in rl:
            continue
        role = rl.index(core)
        got = len(chip_masks(topo, src, rl)[role])
        rid, pid = topo.addr(dst, core)
        m = topo.mask(core, dst)
        for n in (("lu", "qp"), ("ll", "sp"))[role]:
            b = T[n + "%d" % i]
            ap = b[:].bitcast(dt.uint8) if n == "qp" else b[:]
            g.wait_ge(T.sem[n + "%d" % i], got)
            g.remote_dma(ap, ap, remote_sem=T.sem[n + "%d" % i], local_sem=T.sem.out, pid=pid, routing_id=rid,
                         dma_engine_mask=m)
            sent += len(topo.engines(core, dst))
    if sent:
        g.wait_ge(T.sem.out, sent)


def tracker(g, T):
    queues = {"ve": g.vector, "ac": g.scalar, "pe": g.tensor, "gp": g, "sy": g.sync}
    clock = {q: {} for q in queues}
    count = {q: 0 for q in queues}
    snap, acc = {}, {}

    def sync(q, reads, writes):
        req = {}
        for rw, regs in (("r", reads), ("w", writes)):
            for buf, a, b, lane in regs:
                for rw2, a2, b2, lane2, prod, cnt in acc.get(buf, []):
                    if a2 >= b or a >= b2 or (lane is not None and lane2 is not None and lane != lane2):
                        continue
                    if rw == "r" and rw2 == "r" and (buf != "ps" or prod == q):
                        continue
                    req[prod] = max(req.get(prod, 0), cnt)
        for p, n in req.items():
            if clock[q].get(p, 0) >= n:
                continue
            if any(p2 != p and snap[(p2, n2)].get(p, 0) >= n for p2, n2 in req.items()):
                continue
            queues[q].wait_ge(T.sem[p], n)
            for k, x in snap[(p, n)].items():
                clock[q][k] = max(clock[q].get(k, 0), x)

        for p, n in req.items():
            clock[q][p] = max(clock[q].get(p, 0), n)

    def note(prod, cnt, reads, writes):
        for rw, regs in (("r", reads), ("w", writes)):
            for buf, a, b, lane in regs:
                old = acc.get(buf, [])
                if rw == "w":
                    old = [o for o in old if not (a <= o[1] and o[2] <= b and (lane is None or lane == o[3]))]
                else:
                    old = [o for o in old if not (o[0] == "r" and o[4] == prod and a <= o[1] and o[2] <= b
                                                  and (lane is None or lane == o[3]))]
                acc[buf] = old + [(rw, a, b, lane, prod, cnt)]

    def op(q, fn, reads, writes):
        sync(q, reads, writes)
        count[q] += 1
        fn(queues[q]).then_inc(T.sem[q], 1)
        s = dict(clock[q])
        s[q] = count[q]
        snap[(q, count[q])] = s
        note(q, count[q], reads, writes)

    def dma(q, out, in_, reads, writes, sem):
        sync(q, reads, writes)
        queues[q].dma_start(out, in_).then_inc(T.sem[sem], 16)
        s = dict(clock[q])
        s[sem] = 16
        snap[(sem, 16)] = s
        note(sem, 16, reads, writes)

    def arrive(sem, n, writes):
        snap[(sem, n)] = {sem: n}
        note(sem, n, [], writes)

    return op, dma, arrive, sync, count


def reg(buf, a=None, b=None, lane=None):
    return (buf, 0 if a is None else a, 1 << 20 if b is None else b, lane)


def rank_program(g, core, T, topo):
    rank = T.rank_of(core)
    if rank is None:
        relay_program(g, core, T, topo)
        return
    op, dma, arrive, sync, count = tracker(g, T)
    A = AluOpType
    copy = ActivationFunctionType.Copy
    outs = [0]

    def fill(view, value, w):
        op("ve", lambda e: e.memset(view, value), [], [w])

    def iota(view, pattern, base, cm, w, small=False):
        if small:
            op("gp", lambda e: e.iota(view, pattern, base, cm, allow_small_or_imprecise_dtypes=True), [], [w])
        else:
            op("gp", lambda e: e.iota(view, pattern, base, cm), [], [w])

    def ts(out, in0, s1, s2, op0, op1, r, w):
        if op1 is None:
            op("ve", lambda e: e.tensor_scalar(out, in0, s1, None, op0), r, w)
        else:
            op("ve", lambda e: e.tensor_scalar(out, in0, s1, s2, op0, op1), r, w)

    def tt(out, in0, in1, o, r, w):
        op("ve", lambda e: e.tensor_tensor(out, in0, in1, o), r, w)

    def act(out, in_, r, w, scale=None):
        if scale is None:
            op("ac", lambda e: e.activation(out, in_, copy), r, w)
        else:
            op("ac", lambda e: e.activation(out, in_, copy, scale=scale), r, w)

    def quant(qn, sn, a, b, tile, ta, tb):
        op("ve", lambda e: e.quantize_mx(T[qn][:, a:b], T[sn][:, a:b], T[tile][:, 4 * ta:4 * tb]),
           [reg(tile, ta, tb)], [reg(qn, a, b), reg(sn, a, b)])

    def mul(bank, st, s0, mv, m0, m1):
        qs, ss = "q" + st, "s" + st
        qm, sm = "q" + mv, "s" + mv
        n = m1 - m0
        op("pe", lambda e: e.matmul_mx(T.ps[:, 512 * bank:512 * bank + n], T[qs][:, s0:s0 + 128], T[ss][:, s0:s0 + 128],
                                       T[qm][:, m0:m1], T[sm][:, m0:m1], True, True),
           [reg(qs, s0, s0 + 128), reg(ss, s0, s0 + 128), reg(qm, m0, m1), reg(sm, m0, m1)],
           [reg("ps", 512 * bank, 512 * bank + 512)])

    def bank(k):
        return reg("ps", 512 * k, 512 * k + 512)

    def pv(k):
        return T.ps[:, 512 * k:512 * k + H]

    dma("sy", T.x0[:, 0:576], T.x[:, 0:576], [], [reg("x0", 0, H)], "ldxu")
    dma("ac", T.ut[:], T.u[:], [], [reg("ut")], "ldu")
    dma("sy", T.x0[:, 576:1152], T.x[:, 576:1152], [], [reg("x0", H, C)], "ldxl")
    dma("ac", T.mli[:], T.ml[:], [], [reg("mli")], "ldm")
    dma("sy", T.qw[:].bitcast(dt.uint8), T.wc[:], [], [reg("qw")], "ldw")
    dma("ac", T.sw[:], T.ws[:], [], [reg("sw")], "lds")
    dma("sy", T.vt[:], T.v[:], [], [reg("vt")], "ldv")

    iota(T.ul[:], [[16, 8]], 0, 0, reg("ul"))
    iota(T.iom[:], [[1, 448]], 128, -1, reg("iom"))
    iota(T.pc[:], [[0, 9]], 0, 1, reg("pc"))
    iota(T.k16[:], [[16, 9]], 0, 0, reg("k16"))
    iota(T.h[:], [[1, C]], -MID, 0, reg("h"), True)
    iota(T.up[:, H:C], [[1, H]], C - MID, 0, reg("up", H, C), True)
    fill(T.ones[:], 1.0, reg("ones"))
    fill(T.rst[:], 1.0, reg("rst"))
    fill(T.rst[:, 0:448:16], 0.0, reg("rst"))
    fill(T.fl[:], 0.0, reg("fl"))
    fill(T.mg[:, H:H + 16], 0.0, reg("mg", H, H + 16))
    fill(T.lm[:], MID, reg("lm"))
    fill(T.mm[:], 0.0, reg("mm"))
    fill(T.nn[:], float(-MID), reg("nn"))
    op("ve", lambda e: e.tensor_copy(T.uo[:], T.ul[:]), [reg("ul")], [reg("uo")])
    ts(T.ioa[:], T.iom[:], 15, None, A.bitwise_and, None, [reg("iom")], [reg("ioa")])
    ts(T.mskt[:, 0:304], T.ioa[:, 0:304], 0.0, float(H), A.is_equal, A.mult, [reg("ioa", 0, 304)], [reg("mskt", 0, 304)])
    ts(T.mskt[:, 304:448], T.ioa[:, 304:448], 0.0, None, A.is_equal, None, [reg("ioa", 304, 448)], [reg("mskt", 304, 448)])
    ts(T.pd[:], T.pc[:], 15, None, A.bitwise_and, None, [reg("pc")], [reg("pd")])
    tt(T.idl[:], T.pd[:], T.k16[:], A.add, [reg("pd"), reg("k16")], [reg("idl")])
    op("ve", lambda e: e.tensor_copy(T.lm[:, 19:28], T.idl[:]), [reg("idl")], [reg("lm", 19, 28)])
    op("gp", lambda e: e.affine_select(T.idn[:], T.ones[:], [[-1, 128]], A.is_equal, 0.0, 0, 1), [reg("ones")], [reg("idn")])
    iota(T.gtb[:, 0:H], [[1, H]], 0, 0, reg("gtb", 0, H), True)
    iota(T.gtb[:, H:AW], [[1, C]], 0, 0, reg("gtb", H, AW), True)

    op("ve", lambda e: e.quantize_mx(T.qu[:], T.su[:], T.ut[:]), [reg("ut")], [reg("qu"), reg("su")])
    op("ve", lambda e: e.tensor_copy(T.qr[:, 0:128].bitcast(dt.uint32), T.qu[:, 0:128].bitcast(dt.uint32).indirect(T.uo[:, 0:8])),
       [reg("qu"), reg("uo")], [reg("qr")])
    op("ve", lambda e: e.tensor_copy(T.sr[:, 0:128], T.su[:, 0:128].indirect(T.uo[:, 0:8])), [reg("su"), reg("uo")], [reg("sr")])

    def state_half(k, lo):
        a = H if lo else 0

        def planes():
            for b in range(4):
                act(T.xp[:, C * b + a:C * b + a + H], T["x%d" % k][:, 4 * a + b:4 * (a + H):4], [reg("x%d" % k, a, a + H, b)],
                    [reg("xp", C * b + a, C * b + a + H)])
        if 0 < k < ROUNDS:
            planes()
        quant("qx", "sx", a, a + H, "x%d" % k, a, a + H)
        if k < ROUNDS:
            mul(4 + lo, "r", 0, "x", a, a + H)
            if not lo:
                act(T.scu[:], pv(4), [bank(4)], [reg("scu")])
            if k == 0:
                planes()
        else:
            dma("sy", T.oc[:, 4 * a:4 * a + 4 * H], T.qx[:, a:a + H].bitcast(dt.uint8), [reg("qx", a, a + H)], [], "stc%d" % lo)
            mul(4 + lo, "v", 0, "x", a, a + H)
            act(T.ys[:, a:a + H], pv(4 + lo), [bank(4 + lo)], [reg("ys", a, a + H)])
            dma("ac", T.y[:, a:a + H], T.ys[:, a:a + H], [reg("ys", a, a + H)], [], "sty%d" % lo)

    op("ve", lambda e: e.tensor_copy(T.mlf[:, 0:18], T.mli[:]), [reg("mli")], [reg("mlf")])
    ts(T.mlg[:, 0:18], T.mlf[:, 0:18], float(H), float(H), A.is_ge, A.mult, [reg("mlf")], [reg("mlg")])
    tt(T.mlh[:, 0:18], T.mlf[:, 0:18], T.mlg[:, 0:18], A.add, [reg("mlf"), reg("mlg")], [reg("mlh")])
    for a, b in ((0, 0), (10, 9)):
        op("ve", lambda e: e.tensor_copy(T.lm[:, a:a + 9], T.mlh[:, b:b + 9]), [reg("mlh")], [reg("lm", a, a + 9)])
    tt(T.mli2[:, 0:18], T.mlf[:, 0:18], T.mlg[:, 0:18], A.subtract, [reg("mlf"), reg("mlg")], [reg("mli2")])
    for a, b in ((0, 0), (10, 9)):
        ts(T.mm[:, a:a + 9], T.mli2[:, b:b + 9], float(-MID), None, A.add, None, [reg("mli2")], [reg("mm", a, a + 9)])
    state_half(0, 0)
    state_half(0, 1)
    for t in ("ta", "tb", "tc"):
        act(T[t][:, 0:H], T.h[:, 0:H], [reg("h", 0, H)], [reg(t, 0, H)])
        act(T[t][:, C:AW], T.up[:, H:C], [reg("up", H, C)], [reg(t, C, AW)])
    act(T.vtab[:, H:C], T.up[:, H:C], [reg("up", H, C)], [reg("vtab", H, C)])

    def spread(n0, n1, last):
        op("ve", lambda e: e.tensor_tensor_scan(T.sc[:, n0:n1], T.rst[:, n0:n1], T.mg[:, n0:n1], 0.0, A.mult, A.add),
           [reg("rst"), reg("mg", n0, n1)], [reg("sc", n0, n1)])
        buf, w = last
        ts(T[buf][:, 0:w], T.sc[:, n0 + 15:n1:16], float(MID), None, A.add, None, [reg("sc", n0, n1)], [reg(buf, 0, w)])

    def gather(q, out, win, width, off, o0, o1, w, mask=None):
        src = T[win][:, 0:width].indirect(T[off][:, o0:o1])
        r = [reg(win, 0, width), reg(off, o0, o1)]
        if mask is not None:
            tt(out, src, T.msk[:, mask:mask + 16 * (o1 - o0)], A.mult, r + [reg("msk")], [w])
        elif q == "ve":
            op("ve", lambda e: e.tensor_copy(out, src), r, [w])
        else:
            act(out, src, r, [w])

    for i, s in enumerate(STEP):
        x, xn, na, lu, ll = "x%d" % i, "x%d" % (i + 1), "na%d" % i, "lu%d" % i, "ll%d" % i
        qa, qp = "a%d" % i, "p%d" % i
        dst = T.cores[rank ^ s]
        rl = relays(topo, core, dst)
        em = chip_masks(topo, core, rl)
        ids = []
        for k in rl:
            rid, pid = topo.addr(k, core)
            ids.append((rid, pid))
        back = relays(topo, dst, core)
        n_in = [len(topo.engines(k, core)) for k in back]
        arrive(lu, n_in[0], [reg(lu)])
        arrive("q" + qp, n_in[0], [reg("q" + qp)])
        arrive(ll, n_in[1], [reg(ll)])
        arrive("s" + qp, n_in[1], [reg("s" + qp)])

        tt(T.fl[:, 0:H], T.scu[:], pv(5), A.is_gt, [reg("scu"), bank(5)], [reg("fl", 0, H)])
        tt(T.fl[:, C:AW], T.scu[:], pv(5), A.is_le, [reg("scu"), bank(5)], [reg("fl", C, AW)])
        tt(T.mgt[:], T.fl[:, 0:AW].indirect(T.lm[:, 0:28]), T.mskt[:], A.mult, [reg("fl"), reg("lm"), reg("mskt")], [reg("mgt")])
        op("ve", lambda e: e.tensor_tensor_scan(T.sct[:], T.rst[:], T.mgt[:], 0.0, A.mult, A.add),
           [reg("rst"), reg("mgt")], [reg("sct")])
        tt(T.w1[:, 0:19], T.mm[:, 0:19], T.sct[:, 15:304:16], A.add, [reg("mm"), reg("sct")], [reg("w1")])
        tt(T.d1[:, 0:9], T.w1[:, 10:19], T.w1[:, 0:9], A.subtract, [reg("w1")], [reg("d1")])
        tt(T.e1[:, 0:9], T.d1[:, 0:9], T.sct[:, 319:448:16], A.mult, [reg("d1"), reg("sct")], [reg("e1")])
        tt(T.nn[:, 0:9], T.w1[:, 0:9], T.e1[:, 0:9], A.add, [reg("w1"), reg("e1")], [reg("nn", 0, 9)])
        tt(T.nn[:, 10:19], T.w1[:, 10:19], T.e1[:, 0:9], A.subtract, [reg("w1"), reg("e1")], [reg("nn", 10, 19)])
        ts(T[na][:], T.nn[:], float(MID), None, A.add, None, [reg("nn")], [reg(na)])
        sync("gp", [reg(na)], [])
        g.remote_dma_fused([
            RemoteDMATransfer(dst_ids=[DstId(rid=ids[0][0], pnc=ids[0][1])], dma_engine_mask=bits(em[0]),
                              remote_sem=T.sem[lu], src=T[na][:, 0:10], dst=T[lu][:]),
            RemoteDMATransfer(dst_ids=[DstId(rid=ids[1][0], pnc=ids[1][1])], dma_engine_mask=bits(em[1]),
                              remote_sem=T.sem[ll], src=T[na][:, 10:20], dst=T[ll][:])], local_sem=T.sem.out)
        outs[0] += len(em[0]) + len(em[1])
        gather("ac", T.up[:, 0:H], "h", C, na, 10, 19, reg("up", 0, H))

        def z_half(lo):
            a, o = (H, 10) if lo else (0, 0)
            for b in range(4):
                tt(T.z[:, 4 * a + b:4 * (a + H):4], T.xp[:, C * b:C * b + C].indirect(T[na][:, o:o + 9]),
                   T[x][:, 4 * a + b:4 * (a + H):4], A.add, [reg(x, a, a + H, b), reg("xp", C * b, C * b + C), reg(na, o, o + 9)],
                   [reg("z", a, a + H, b)])
            quant("qz", "sz", a, a + H, "z", a, a + H)

        def a_half(lo):
            a, k = (H, 0) if lo else (0, 4)
            for b in range(4):
                mul(k + b, "w", 128 * b, "z", a, a + H)
            for b in range(4):
                act(T.a[:, 4 * a + b:4 * (a + H):4], pv(k + b), [bank(k + b)], [reg("a", a, a + H, b)], scale=0.015625)

        z_half(1)
        a_half(1)
        z_half(0)
        a_half(0)
        quant("q" + qa, "s" + qa, H, C, "a", H, C)
        for n, k, view in (("q", 0, T["q" + qa][:, H:C].bitcast(dt.uint8)), ("s", 1, T["s" + qa][:, H:C])):
            sync("gp", [reg(n + qa, H, C)], [])
            land = T[n + qp][:].bitcast(dt.uint8) if n == "q" else T[n + qp][:]
            g.remote_dma(land, view, remote_sem=T.sem[n + qp], local_sem=T.sem.out, pid=ids[k][1], routing_id=ids[k][0],
                         dma_engine_mask=bits(em[k]))
            outs[0] += len(em[k])
        if i == 0:
            ts(T.msk[:], T.ioa[:, 0:304], 0.0, None, A.is_equal, None, [reg("ioa", 0, 304)], [reg("msk")])
            fill(T.et[:], 0.0, reg("et"))
            for b in range(4):
                op("ve", lambda e: e.tensor_copy(T.et[:, 513 * b:512 * b + 512:4], T.idn[:]), [reg("idn"), reg("et", 128 * b, 128 * b + 128)],
                   [reg("et", 128 * b, 128 * b + 128, b)])
            op("ve", lambda e: e.quantize_mx(T.qe[:], T.se[:], T.et[:]), [reg("et")], [reg("qe"), reg("se")])
        quant("q" + qa, "s" + qa, 0, H, "a", 0, H)
        if i == 0:
            op("ve", lambda e: e.quantize_mx(T.qv[:], T.sv[:], T.vt[:]), [reg("vt")], [reg("qv"), reg("sv")])
            for b in range(4):
                fill(T.db[:, AW * b + H:AW * b + C], 0.0, reg("db", AW * b + H, AW * b + C))
        for b in range(4):
            mul(b, "e", 128 * b, qa, 0, H)
        for b in range(4):
            act(T.db[:, AW * b:AW * b + H], pv(b), [bank(b)], [reg("db", AW * b, AW * b + H)])
        for b in range(4):
            mul(4 + b, "e", 128 * b, qp, 0, H)

        def table(t):
            return T[t][:, H:C], reg(t, H, C)
        mgu, mgl = (T.mg[:, 0:H], reg("mg", 0, H)), (T.mg[:, 160:304], reg("mg", 160, 304))
        gather("ve", mgu[0], "up", C, lu, 0, 9, mgu[1], 0)
        v, w = table("ta")
        gather("ac", v, "up", C, lu, 0, 9, w)
        spread(0, H, ("lk0", 9))
        v, w = table("tb")
        gather("ve", v, "ta", AW, "lk0", 0, 9, w)
        now, lk = "tb", 0
        for t in ("tc", "ta", "tb", "tc"):
            gather("ve", mgu[0], now, AW, "lk%d" % lk, 0, 9, mgu[1], 0)
            v, w = table(t)
            gather("ac", v, now, AW, "lk%d" % lk, 0, 9, w)
            lk = 1 - lk
            spread(0, H, ("lk%d" % lk, 9))
            now = t
        for t in ("ta", "tb"):
            v, w = table(t)
            gather("ve", v, now, AW, "lk%d" % lk, 0, 9, w)
            now = t
        gather("ac", T.vtab[:, 0:H], now, AW, na, 10, 19, reg("vtab", 0, H))
        gather("ve", mgu[0], now, AW, na, 0, 9, mgu[1], 0)
        gather("ve", mgl[0], "vtab", C, ll, 0, 9, mgl[1], 160)
        spread(0, 304, ("lm", 19))
        for b in range(4):
            act(T.db[:, AW * b + C:AW * b + AW], pv(4 + b), [bank(4 + b)], [reg("db", AW * b + C, AW * b + AW)])
        if i + 1 == ROUNDS:
            gather("ac", T.mrow[:], "gtb", AW, "lm", 0, 19, reg("mrow"))
            dma("sy", T.mo[:, 0:H], T.mrow[0:128:16, 0:H], [reg("mrow")], [], "stm0")
            dma("sy", T.mo[:, H:C], T.mrow[0:128:16, 160:304], [reg("mrow")], [], "stm1")
        for lo in (0, 1):
            a, o = (H, 10) if lo else (0, 0)
            for b in range(4):
                tt(T[xn][:, 4 * a + b:4 * (a + H):4], T.db[:, AW * b:AW * b + AW].indirect(T.lm[:, o:o + 9]),
                   T[x][:, 4 * a + b:4 * (a + H):4], A.add, [reg("db", AW * b, AW * b + AW), reg("lm", o, o + 9), reg(x, a, a + H, b)],
                   [reg(xn, a, a + H, b)])
            state_half(i + 1, lo)
        if i + 1 < ROUNDS:
            sv = T.sc[:, 15:304:16]
            ts(T.mt[:, 0:19], sv, 0.0, float(-C), A.is_ge, A.mult, [reg("sc")], [reg("mt")])
            tt(T.mm[:, 0:19], T.mt[:, 0:19], sv, A.add, [reg("mt"), reg("sc")], [reg("mm")])
    for k in range(4):
        dma("sy" if k % 2 else "ac", T.osc[4 * k:4 * k + 4, :], T.sx[32 * k:32 * k + 4, :], [reg("sx")], [], "sts%d" % k)
    for n in ("ve", "ac", "pe", "gp"):
        g.wait_ge(T.sem[n], count[n])
    for n in LOADS + STORES:
        g.wait_ge(T.sem[n], 16)
    g.wait_ge(T.sem.out, outs[0])
